import numpy as np
import ml_dtypes


def mxq(x, axis, fmt="e4m3"):
    dtype, down = {"e4m3": (ml_dtypes.float8_e4m3fn, 7), "e5m2": (ml_dtypes.float8_e5m2, 14)}[fmt]
    v = np.moveaxis(np.asarray(x, np.float32).astype(ml_dtypes.bfloat16).astype(np.float64), axis, -1)
    blocks = v.reshape(v.shape[:-1] + (-1, 32))
    amax = np.abs(blocks).max(-1, keepdims=True)
    byte = np.maximum(np.where(amax > 0, np.frexp(amax)[1] - 1 + 127, 0) - down, 1)
    scale = np.exp2(byte - 127.0)
    codes = (blocks / scale).astype(np.float32).astype(dtype).astype(np.float64)
    return np.moveaxis((codes * scale).reshape(v.shape), -1, axis)


WIDE = False


def mx_kscale(k):
    if not WIDE:
        return np.ones(k)
    levels = np.array([10, -10, 5, -5, 0])
    if k % 512:
        return np.exp2(np.random.permutation(np.resize(levels, k // 32))).repeat(32)
    a = np.empty((k // 512, 16))
    for p in range(k // 512):
        a[p, :8] = np.random.permutation(np.resize(levels, 8))
        for g in range(8):
            far = levels[np.abs(levels - a[p, g]) >= 10]
            a[p, g + 8] = far[np.random.randint(len(far))]
    return np.exp2(a.ravel()).repeat(32)


def f64(x):
    return np.asarray(x).astype(np.float64)


def striped(idx):
    return np.tile(idx.reshape(-1, 16).T, (8, 1)).astype(np.uint16)


def unstriped(offs):
    return offs[:16].T.reshape(-1).astype(np.int64)


def pack_weight(w):
    k, n = w.shape
    w = f64(np.asarray(w, np.float32).astype(ml_dtypes.bfloat16)).reshape(k // 32, 32, n)
    amax = np.abs(w).max(1)
    byte = np.clip(np.where(amax > 0, np.frexp(amax)[1] - 1 + 127 - 7, 1), 1, 254)
    scaled = (w * np.exp2(127.0 - byte)[:, None, :]).reshape(k, n).astype(np.float32)
    words = np.ascontiguousarray(scaled.reshape(k // 512, 128, 4, n).transpose(0, 1, 3, 2)).astype(ml_dtypes.float8_e4m3fn).view(np.uint8)
    return words, np.ascontiguousarray(byte.astype(np.uint8).reshape(k // 512, 16, n))


def unpack_weight(words, scales):
    g, p, n, _ = words.shape
    vals = np.ascontiguousarray(words).view(ml_dtypes.float8_e4m3fn).astype(np.float64) * np.repeat(np.exp2(scales.astype(np.float64) - 127.0), 8, axis=1)[..., None]
    return vals.transpose(0, 1, 3, 2).reshape(g * 512, n)


def relu(v):
    return np.maximum(v, 0.0)


K, T, S, D, N, H = 512, 2048, 1024, 4, 128, 512


def setup_inputs():
    n = np.random.standard_normal
    s = mx_kscale(K)[:, None]
    u = mx_kscale(H)
    packed_xT = pack_weight(n((K, T)) * s)
    return {
        "x_words": packed_xT[0],
        "x_scales": packed_xT[1],
        "w1": (n((K, H)) / np.sqrt(K) / s).astype(np.float32),
        "w2": (n((K, H)) / np.sqrt(K) / s).astype(np.float32),
        "sat": (np.random.uniform(0.5, 1.2, (H, S))).astype(np.float32),
        "unit": (np.random.uniform(0.6, 1.4, (H, 1)) * u[:, None]).astype(np.float32),
        "w3": (n((H, N)) / np.sqrt(H) / u[:, None]).astype(np.float32),
        "offs": striped(np.random.permutation(T)[:S]),
        "dsn": striped(np.random.permutation(S)),
    }


def reference(x_words, x_scales, w1, w2, sat, unit, w3, offs, dsn):
    xq = unpack_weight(x_words, x_scales)[:, unstriped(offs)]
    qe = mxq(f64(w1), 0, "e4m3").T @ xq
    queue = np.log(np.exp(qe) + 1.0)
    qd = queue[:, unstriped(dsn)]
    pres = queue - (0.8 * qd)
    ps_ = relu(pres) * f64(sat)
    phase = ps_.reshape(len(ps_), -1, D).sum(axis=2)
    green = phase / (phase + 1.5)
    oc = mxq(f64(w2), 0, "e4m3").T @ xq
    occ = np.log(np.exp(oc) + 1.0)
    serv = np.minimum(queue, 1.2 * (np.repeat(green, D, axis=1) * occ))
    sd = serv[:, unstriped(dsn)]
    qnew = queue - serv + 0.5 * sd
    hid = f64(unit) * (qnew - (0.3 * occ))
    return mxq(f64(w3), 0, "e4m3").T @ mxq(hid, 0, "e4m3")

@@ -1,0 +1,216 @@
+from contextlib import ExitStack
+
+import concourse.mybir as mybir
+from concourse.masks import make_identity
+
+K, T, S, D, N, H = 512, 2048, 1024, 4, 128, 512
+FLOPS = 2 * K * H * S * 2 + 2 * H * N * S
+
+F32 = mybir.dt.float32
+BF16 = mybir.dt.bfloat16
+I32 = mybir.dt.int32
+U32 = mybir.dt.uint32
+U16 = mybir.dt.uint16
+U8 = mybir.dt.uint8
+FP8X4 = mybir.dt.float8_e4m3fn_x4
+ALU = mybir.AluOpType
+ACT = mybir.ActivationFunctionType
+AXIS = mybir.AxisListType
+
+P = 128
+PACK = 4
+HALF = S // 2
+COLS = HALF // 16
+V = S // D
+TINY = 2.0 ** -63
+
+
+def tile_picked_ytraffs_queue_p_kernel(tc, x_words, x_scales, w1, w2, sat, unit, w3, offs, dsn, out):
+    nc = tc.nc
+    with ExitStack() as ctx:
+        keep = ctx.enter_context(tc.tile_pool(name="keep", bufs=1))
+        work = ctx.enter_context(tc.tile_pool(name="work", bufs=2))
+        psum = ctx.enter_context(tc.psum_pool(name="psum", bufs=1))
+
+        def bank(b):
+            return psum.tile([P, 512], F32, name="bank%d" % b, tag="bank%d" % b)
+
+        def halves(ap, h):
+            return ap[:, h * HALF : (h + 1) * HALF]
+
+        xs_all = keep.tile([P, T], U8, name="xs_all")
+        nc.vector.memset(xs_all[:].bitcast(I32), 0)
+        offs_t = keep.tile([P, S // 16], U16, name="offs_t")
+        nc.sync.dma_start(offs_t[:], offs)
+        for q in range(4):
+            nc.sync.dma_start(xs_all[32 * q : 32 * q + 4, :].bitcast(I32), x_scales[0, 4 * q : 4 * q + 4, :].bitcast(I32))
+        w1_raw = keep.tile([P, PACK, H], F32, name="w1_raw")
+        nc.sync.dma_start(w1_raw[:], w1.rearrange("(p j) c -> p j c", j=PACK))
+        xw_all = keep.tile([P, T], I32, name="xw_all")
+        nc.sync.dma_start(xw_all[:], x_words[0].rearrange("p n t -> p (n t)").bitcast(I32))
+        w2_raw = keep.tile([P, PACK, H], F32, name="w2_raw")
+        nc.sync.dma_start(w2_raw[:], w2.rearrange("(p j) c -> p j c", j=PACK))
+        dsn_t = keep.tile([P, S // 16], U16, name="dsn_t")
+        nc.sync.dma_start(dsn_t[:], dsn)
+        sat_rows = sat.rearrange("(p t) j -> p t j", t=PACK)
+        sat_t = [keep.tile([P, S], F32, name="sat%d" % t) for t in range(PACK)]
+        for t in (2, 3, 0, 1):
+            nc.sync.dma_start(sat_t[t][:], sat_rows[:, t, :])
+        w3_raw = keep.tile([P, PACK, N], F32, name="w3_raw")
+        nc.sync.dma_start(w3_raw[:], w3.rearrange("(p j) c -> p j c", j=PACK))
+        unit_row = keep.tile([P, H], F32, name="unit_row")
+        nc.sync.dma_start(unit_row[:], unit.rearrange("h o -> (h o)").partition_broadcast(P))
+
+        ident = keep.tile([P, P], F32, name="ident")
+        make_identity(nc, ident[:])
+
+        xw = [keep.tile([P, HALF], U32, name="xw%d" % h, align_bytes=64) for h in range(2)]
+        xs = [keep.tile([P, HALF], U8, name="xs%d" % h, align_bytes=64) for h in range(2)]
+
+        def pick_scales(h):
+            nc.vector.tensor_copy(xs[h][:], xs_all[:].indirect(offs_t[:, h * COLS : (h + 1) * COLS]))
+
+        def pick_words(h):
+            nc.vector.tensor_copy(xw[h][:], xw_all[:].bitcast(U32).indirect(offs_t[:, h * COLS : (h + 1) * COLS]))
+
+        def dealt_views(raw, grouped, mh):
+            dst = grouped[:].rearrange("p (t m j) -> p m j t", t=PACK, j=PACK)[:, 64 * mh : 64 * mh + 64]
+            src = raw[:].rearrange("p j (m t) -> p m j t", t=PACK)[:, 64 * mh : 64 * mh + 64]
+            return dst, src
+
+        def quantize(grouped, width, label):
+            codes = keep.tile([P, width], U32, name=label + "_codes", align_bytes=64)
+            scales = keep.tile([P, width], U8, name=label + "_scales", align_bytes=64)
+            nc.vector.quantize_mx(out=codes[:].bitcast(FP8X4), scales=scales[:], in_=grouped)
+            return codes, scales
+
+        pick_scales(0)
+        w1_bf = keep.tile([P, PACK * H], BF16, name="w1_bf", align_bytes=64)
+        nc.scalar.copy(*dealt_views(w1_raw, w1_bf, 0))
+        nc.vector.tensor_copy(*dealt_views(w1_raw, w1_bf, 1))
+        w1_q = quantize(w1_bf[:], H, "w1")
+        pick_words(0)
+        pick_scales(1)
+        pick_words(1)
+
+        def product(wq, t, h):
+            acc = bank(2 * t + h)
+            cols = slice(P * t, P * (t + 1))
+            nc.tensor.matmul_mx(out=acc[:], lhsT=wq[0][:, cols].bitcast(FP8X4), lhsT_scale=wq[1][:, cols],
+                                rhs=xw[h][:].bitcast(FP8X4), rhs_scale=xs[h][:], start=True, stop=True)
+            return acc
+
+        logs = [keep.tile([P, S], F32, name="logs%d" % t) for t in range(PACK)]
+
+        def sigmoids(wq):
+            accs = {}
+            for h in range(2):
+                for t in range(PACK):
+                    accs[t, h] = product(wq, t, h)
+                    nc.scalar.activation(halves(logs[t], h), accs[t, h][:], ACT.Sigmoid, scale=-1.0)
+            return accs
+
+        def logarithm(t):
+            nc.scalar.activation(logs[t][:], logs[t][:], ACT.Ln, bias=TINY)
+
+        def softplus_end(dst, accs, t):
+            for h in range(2):
+                nc.vector.scalar_tensor_tensor(halves(dst, h), halves(logs[t], h), -1.0, accs[t, h][:], ALU.mult, ALU.max)
+
+        def lanes(h):
+            return dsn_t[:, h * COLS : (h + 1) * COLS]
+
+        qe = sigmoids(w1_q)
+
+        w2_bf = keep.tile([P, PACK * H], BF16, name="w2_bf", align_bytes=64)
+        for mh in range(2):
+            nc.vector.tensor_copy(*dealt_views(w2_raw, w2_bf, mh))
+        w2_q = quantize(w2_bf[:], H, "w2")
+        w3_bf = keep.tile([P, N, PACK], BF16, name="w3_bf", align_bytes=64)
+        nc.vector.tensor_copy(w3_bf[:], w3_raw[:].rearrange("p j m -> p m j"))
+        w3_q = quantize(w3_bf[:].rearrange("p m j -> p (m j)"), N, "w3")
+
+        queue = [keep.tile([P, S], F32, name="queue%d" % t) for t in range(PACK)]
+        for t in range(PACK):
+            logarithm(t)
+            softplus_end(queue[t], qe, t)
+
+        phase = keep.tile([P, PACK, V], F32, name="phase")
+        gap = [keep.tile([P, S], F32, name="gap%d" % t) for t in range(PACK)]
+        for t in (0, 1):
+            for h in range(2):
+                nc.scalar.activation(halves(gap[t], h), queue[t][:].indirect(lanes(h)), ACT.Copy)
+
+        def phase_of(t):
+            nc.vector.scalar_tensor_tensor(gap[t][:], gap[t][:], 0.0, sat_t[t][:], ALU.min, ALU.mult)
+            nc.vector.tensor_reduce(phase[:, t, :], gap[t][:].rearrange("p (v d) -> p v d", d=D), AXIS.X, ALU.add)
+
+        for t in (2, 3):
+            own = work.tile([P, S], F32, name="own")
+            nc.vector.tensor_scalar(own[:], queue[t][:], 1.25, None, ALU.mult)
+            for h in range(2):
+                nc.vector.tensor_tensor(halves(gap[t], h), queue[t][:].indirect(lanes(h)), halves(own, h), ALU.subtract)
+            phase_of(t)
+        for t in (0, 1):
+            nc.vector.scalar_tensor_tensor(gap[t][:], queue[t][:], -1.25, gap[t][:], ALU.mult, ALU.add)
+            phase_of(t)
+
+        oc = sigmoids(w2_q)
+        for t in range(PACK):
+            logarithm(t)
+
+        green = keep.tile([P, PACK, V], F32, name="green")
+        nc.scalar.activation(green[:], phase[:], ACT.Ln, scale=-0.8 / 1.5, bias=TINY)
+        for u in range(2):
+            nc.scalar.activation(green[:, 2 * u : 2 * u + 2, :], green[:, 2 * u : 2 * u + 2, :], ACT.Sigmoid)
+
+        occ = [keep.tile([P, S], F32, name="occ%d" % t) for t in range(PACK)]
+        for t in range(PACK):
+            softplus_end(occ[t], oc, t)
+
+        unserved = [keep.tile([P, S], F32, name="unserved%d" % t) for t in range(PACK)]
+        occ_part = logs
+        arrive = gap
+        for t in range(PACK):
+            flow = work.tile([P, S], F32, name="flow")
+            nc.vector.scalar_tensor_tensor(
+                flow[:].rearrange("p (v d) -> p v d", d=D), green[:, t, :].unsqueeze(2).to_broadcast([P, V, D]), -1.2,
+                occ[t][:].rearrange("p (v d) -> p v d", d=D), ALU.mult, ALU.mult)
+            nc.vector.scalar_tensor_tensor(unserved[t][:], queue[t][:], -1.0, flow[:], ALU.mult, ALU.max)
+            for h in range(2):
+                nc.scalar.activation(halves(arrive[t], h), unserved[t][:].indirect(lanes(h)), ACT.Copy, scale=-0.5)
+            nc.vector.tensor_scalar(occ_part[t][:], occ[t][:], -0.3, None, ALU.mult)
+
+        hid_t = [keep.tile([P, 8, P, 2], BF16, name="hid_t%d" % u) for u in range(2)]
+        words = {}
+        for u in range(2):
+            sums = [bank(4 * u + k) for k in range(4)]
+            steps = [(terms, e) for terms in (queue, occ_part) for e in range(2)] + [(terms, e) for e in range(2) for terms in (unserved, arrive)]
+            for n, (terms, e) in enumerate(steps):
+                for k in range(4):
+                    for b in range(2):
+                        blk = 2 * k + b
+                        nc.tensor.matmul(sums[k][:, (2 * b + e) * P : (2 * b + e + 1) * P], terms[2 * u + e][:, blk * P : (blk + 1) * P], ident[:],
+                                         start=(n == 0 and b == 0), stop=(n == len(steps) - 1 and b == 1), is_transpose=True)
+            unit_u = unit_row[:].rearrange("l (p u e) -> l u p e", u=2, e=2)[:, u]
+            for k in range(4):
+                nc.vector.tensor_tensor(hid_t[u][:, 2 * k : 2 * k + 2], sums[k][:].rearrange("l (b e p) -> l b p e", b=2, e=2),
+                                        unit_u.unsqueeze(1).to_broadcast([P, 2, P, 2]), ALU.mult)
+                if u == 0:
+                    words[k] = bank(k)
+                pairs = hid_t[u][:].rearrange("l b p e -> l (b p e)").bitcast(F32)
+                for b in range(2):
+                    blk = 2 * k + b
+                    nc.tensor.transpose(words[k][:, (2 * u + b) * P : (2 * u + b + 1) * P], pairs[:, blk * P : (blk + 1) * P], ident[:])
+
+        Q = S // 4
+        for k in range(4):
+            hid = work.tile([P, Q * PACK], BF16, name="hid", align_bytes=64)
+            nc.scalar.copy(hid[:].bitcast(F32).rearrange("p (l u) -> p l u", u=2), words[k][:].rearrange("p (u l) -> p l u", u=2))
+            codes, scales = quantize(hid[:], Q, "hid%d" % k)
+            acc = bank(4 + k)
+            nc.tensor.matmul_mx(out=acc[:, 0:Q], lhsT=w3_q[0][:].bitcast(FP8X4), lhsT_scale=w3_q[1][:],
+                                rhs=codes[:].bitcast(FP8X4), rhs_scale=scales[:], start=True, stop=True)
+            res = work.tile([P, Q], F32, name="res")
+            nc.scalar.copy(res[:], acc[:, 0:Q])
+            nc.sync.dma_start(out[:, k * Q : (k + 1) * Q], res[:])

@@ -38,6 +38,21 @@ def tile_picked_ytraffs_queue_p_kernel(tc, x_words, x_scales, w1, w2, sat, unit,
         def halves(ap, h):
             return ap[:, h * HALF : (h + 1) * HALF]
 
+        ORDER = (2, 3, 0, 1)
+        UORD = (1, 0)
+        MERGED = (0, 1)
+        sc, vc = nc.scalar.copy, nc.vector.tensor_copy
+        WCOPY = [sc]*4
+        RCOPY = [sc]*4
+        FUSED = (2, 3)
+        OWN_ENG = nc.vector
+        def part_v(dst, src):
+            nc.vector.tensor_scalar(dst, src, -0.3, None, ALU.mult)
+        def part_s(dst, src):
+            nc.scalar.activation(dst, src, ACT.Copy, scale=-0.3)
+        def part_g(dst, src):
+            nc.gpsimd.tensor_scalar(dst, src, -0.3, 0.0, ALU.mult, ALU.add)
+        PART_ENG = [part_g]*4
         xs_all = keep.tile([P, T], U8, name="xs_all")
         nc.vector.memset(xs_all[:].bitcast(I32), 0)
         offs_t = keep.tile([P, S // 16], U16, name="offs_t")
@@ -93,8 +108,8 @@ def tile_picked_ytraffs_queue_p_kernel(tc, x_words, x_scales, w1, w2, sat, unit,
         pick_scales(1)
         pick_words(1)
 
-        def product(wq, t, h):
-            acc = bank(2 * t + h)
+        def product(wq, t, h, b):
+            acc = bank(b)
             cols = slice(P * t, P * (t + 1))
             nc.tensor.matmul_mx(out=acc[:], lhsT=wq[0][:, cols].bitcast(FP8X4), lhsT_scale=wq[1][:, cols],
                                 rhs=xw[h][:].bitcast(FP8X4), rhs_scale=xs[h][:], start=True, stop=True)
@@ -105,8 +120,8 @@ def tile_picked_ytraffs_queue_p_kernel(tc, x_words, x_scales, w1, w2, sat, unit,
         def sigmoids(wq):
             accs = {}
             for h in range(2):
-                for t in range(PACK):
-                    accs[t, h] = product(wq, t, h)
+                for t in ORDER:
+                    accs[t, h] = product(wq, t, h, 2 * t + h)
                     nc.scalar.activation(halves(logs[t], h), accs[t, h][:], ACT.Sigmoid, scale=-1.0)
             return accs
 
@@ -131,86 +146,119 @@ def tile_picked_ytraffs_queue_p_kernel(tc, x_words, x_scales, w1, w2, sat, unit,
         w3_q = quantize(w3_bf[:].rearrange("p m j -> p (m j)"), N, "w3")
 
         queue = [keep.tile([P, S], F32, name="queue%d" % t) for t in range(PACK)]
-        for t in range(PACK):
+        own = {t: keep.tile([P, S], F32, name="own%d" % t) for t in FUSED}
+        for t in ORDER:
             logarithm(t)
             softplus_end(queue[t], qe, t)
+            if t in FUSED:
+                OWN_ENG.tensor_scalar(own[t][:], queue[t][:], 1.25, 0.0, ALU.mult, ALU.add)
 
-        phase = keep.tile([P, PACK, V], F32, name="phase")
+        press = [keep.tile([P, D, V], F32, name="press%d" % t) for t in range(PACK)]
         gap = [keep.tile([P, S], F32, name="gap%d" % t) for t in range(PACK)]
-        for t in (0, 1):
-            for h in range(2):
-                nc.scalar.activation(halves(gap[t], h), queue[t][:].indirect(lanes(h)), ACT.Copy)
-
-        def phase_of(t):
-            nc.vector.scalar_tensor_tensor(gap[t][:], gap[t][:], 0.0, sat_t[t][:], ALU.min, ALU.mult)
-            nc.vector.tensor_reduce(phase[:, t, :], gap[t][:].rearrange("p (v d) -> p v d", d=D), AXIS.X, ALU.add)
-
-        for t in (2, 3):
-            own = work.tile([P, S], F32, name="own")
-            nc.vector.tensor_scalar(own[:], queue[t][:], 1.25, None, ALU.mult)
-            for h in range(2):
-                nc.vector.tensor_tensor(halves(gap[t], h), queue[t][:].indirect(lanes(h)), halves(own, h), ALU.subtract)
-            phase_of(t)
-        for t in (0, 1):
-            nc.vector.scalar_tensor_tensor(gap[t][:], queue[t][:], -1.25, gap[t][:], ALU.mult, ALU.add)
-            phase_of(t)
+        for t in ORDER:
+            if t not in FUSED:
+                for h in range(2):
+                    nc.scalar.activation(halves(gap[t], h), queue[t][:].indirect(lanes(h)), ACT.Copy)
+        for t in ORDER:
+            if t in FUSED:
+                for h in range(2):
+                    nc.vector.tensor_tensor(halves(gap[t], h), queue[t][:].indirect(lanes(h)), halves(own[t], h), ALU.subtract)
+            else:
+                nc.vector.scalar_tensor_tensor(gap[t][:], queue[t][:], -1.25, gap[t][:], ALU.mult, ALU.add)
+            nc.vector.scalar_tensor_tensor(press[t][:].rearrange("p d v -> p v d"), gap[t][:].rearrange("p (v d) -> p v d", d=D), 0.0,
+                                           sat_t[t][:].rearrange("p (v d) -> p v d", d=D), ALU.min, ALU.mult)
 
         oc = sigmoids(w2_q)
-        for t in range(PACK):
+        for t in ORDER:
             logarithm(t)
 
-        green = keep.tile([P, PACK, V], F32, name="green")
-        nc.scalar.activation(green[:], phase[:], ACT.Ln, scale=-0.8 / 1.5, bias=TINY)
-        for u in range(2):
-            nc.scalar.activation(green[:, 2 * u : 2 * u + 2, :], green[:, 2 * u : 2 * u + 2, :], ACT.Sigmoid)
+        phase = [bank(b) for b in range(2)]
+        for n, t in enumerate(ORDER):
+            for d in range(D):
+                for b in range(2):
+                    nc.tensor.matmul(phase[b][:, t * P : (t + 1) * P], press[t][:, d, b * P : (b + 1) * P], ident[:],
+                                     start=(n == 0 and d == 0), stop=(n == PACK - 1 and d == D - 1), is_transpose=True)
+        shared = keep.tile([P, 2 * S], F32, name="shared")
+        green_t = shared[:, HALF : HALF + S].rearrange("p (b i) -> p b i", b=2)
+        for b in range(2):
+            nc.scalar.activation(green_t[:, b, :], phase[b][:], ACT.Ln, scale=-0.8 / 1.5, bias=TINY)
+        green = {}
+        for u in UORD:
+            pair = green_t[:, :, 2 * u * P : (2 * u + 2) * P]
+            nc.scalar.activation(pair, pair, ACT.Sigmoid)
+            green[u] = bank(u)
+            for e in range(2):
+                for b in range(2):
+                    nc.tensor.transpose(green[u][:, (2 * e + b) * P : (2 * e + b + 1) * P], green_t[:, b, (2 * u + e) * P : (2 * u + e + 1) * P], ident[:])
 
         occ = [keep.tile([P, S], F32, name="occ%d" % t) for t in range(PACK)]
-        for t in range(PACK):
+        occ_part = [logs[t][:] for t in range(PACK)]
+        for t in ORDER:
+            if t < 2:
+                for h in range(2):
+                    oc[t, h] = product(w2_q, t, h, 4 + 2 * t + h)
             softplus_end(occ[t], oc, t)
+            if t in MERGED:
+                nc.vector.scalar_tensor_tensor(occ_part[t], occ[t][:], -0.3, queue[t][:], ALU.mult, ALU.add)
+            else:
+                PART_ENG[t](occ_part[t], occ[t][:])
 
         unserved = [keep.tile([P, S], F32, name="unserved%d" % t) for t in range(PACK)]
-        occ_part = logs
         arrive = gap
-        for t in range(PACK):
+        for t in ORDER:
             flow = work.tile([P, S], F32, name="flow")
-            nc.vector.scalar_tensor_tensor(
-                flow[:].rearrange("p (v d) -> p v d", d=D), green[:, t, :].unsqueeze(2).to_broadcast([P, V, D]), -1.2,
-                occ[t][:].rearrange("p (v d) -> p v d", d=D), ALU.mult, ALU.mult)
-            nc.vector.scalar_tensor_tensor(unserved[t][:], queue[t][:], -1.0, flow[:], ALU.mult, ALU.max)
+            for h in range(2):
+                share = green[t // 2][:, (t % 2) * V + h * P : (t % 2) * V + (h + 1) * P]
+                nc.vector.scalar_tensor_tensor(
+                    halves(flow, h).rearrange("p (v d) -> p v d", d=D), share.unsqueeze(2).to_broadcast([P, P, D]), -1.2,
+                    halves(occ[t], h).rearrange("p (v d) -> p v d", d=D), ALU.mult, ALU.mult)
+            for h in range(2):
+                nc.vector.scalar_tensor_tensor(halves(unserved[t], h), halves(queue[t], h), -1.0, halves(flow, h), ALU.mult, ALU.max)
             for h in range(2):
                 nc.scalar.activation(halves(arrive[t], h), unserved[t][:].indirect(lanes(h)), ACT.Copy, scale=-0.5)
-            nc.vector.tensor_scalar(occ_part[t][:], occ[t][:], -0.3, None, ALU.mult)
 
         hid_t = [keep.tile([P, 8, P, 2], BF16, name="hid_t%d" % u) for u in range(2)]
         words = {}
-        for u in range(2):
-            sums = [bank(4 * u + k) for k in range(4)]
-            steps = [(terms, e) for terms in (queue, occ_part) for e in range(2)] + [(terms, e) for e in range(2) for terms in (unserved, arrive)]
-            for n, (terms, e) in enumerate(steps):
+        first, second = UORD
+        sum_banks = {first: (2, 3, 4, 5), second: (6, 7, first, second)}
+        Q = S // 4
+        for u in UORD:
+            sums = [bank(b) for b in sum_banks[u]]
+
+            def add_turned(terms, e, k, start=False, stop=False):
+                for b in range(2):
+                    blk = 2 * k + b
+                    nc.tensor.matmul(sums[k][:, (2 * b + e) * P : (2 * b + e + 1) * P], terms[2 * u + e][:, blk * P : (blk + 1) * P], ident[:],
+                                     start=start and b == 0, stop=stop and b == 1, is_transpose=True)
+
+            for k in range(4):
+                for e in range(2):
+                    if 2 * u + e not in MERGED:
+                        add_turned(queue, e, k, start=(e == 0))
+            for e in range(2):
                 for k in range(4):
-                    for b in range(2):
-                        blk = 2 * k + b
-                        nc.tensor.matmul(sums[k][:, (2 * b + e) * P : (2 * b + e + 1) * P], terms[2 * u + e][:, blk * P : (blk + 1) * P], ident[:],
-                                         start=(n == 0 and b == 0), stop=(n == len(steps) - 1 and b == 1), is_transpose=True)
+                    add_turned(occ_part, e, k, start=(e == 0 and 2 * u in MERGED))
+            for e in range(2):
+                for k in range(4):
+                    add_turned(unserved, e, k)
+                    add_turned(arrive, e, k, stop=(e == 1))
             unit_u = unit_row[:].rearrange("l (p u e) -> l u p e", u=2, e=2)[:, u]
             for k in range(4):
                 nc.vector.tensor_tensor(hid_t[u][:, 2 * k : 2 * k + 2], sums[k][:].rearrange("l (b e p) -> l b p e", b=2, e=2),
                                         unit_u.unsqueeze(1).to_broadcast([P, 2, P, 2]), ALU.mult)
-                if u == 0:
-                    words[k] = bank(k)
+                if u == first:
+                    words[k] = bank(sum_banks[first][k])
                 pairs = hid_t[u][:].rearrange("l b p e -> l (b p e)").bitcast(F32)
                 for b in range(2):
                     blk = 2 * k + b
                     nc.tensor.transpose(words[k][:, (2 * u + b) * P : (2 * u + b + 1) * P], pairs[:, blk * P : (blk + 1) * P], ident[:])
-
-        Q = S // 4
-        for k in range(4):
-            hid = work.tile([P, Q * PACK], BF16, name="hid", align_bytes=64)
-            nc.scalar.copy(hid[:].bitcast(F32).rearrange("p (l u) -> p l u", u=2), words[k][:].rearrange("p (u l) -> p l u", u=2))
-            codes, scales = quantize(hid[:], Q, "hid%d" % k)
-            acc = bank(4 + k)
-            nc.tensor.matmul_mx(out=acc[:, 0:Q], lhsT=w3_q[0][:].bitcast(FP8X4), lhsT_scale=w3_q[1][:],
-                                rhs=codes[:].bitcast(FP8X4), rhs_scale=scales[:], start=True, stop=True)
-            res = work.tile([P, Q], F32, name="res")
-            nc.scalar.copy(res[:], acc[:, 0:Q])
-            nc.sync.dma_start(out[:, k * Q : (k + 1) * Q], res[:])
+                if u == second:
+                    hid = keep.tile([P, Q * PACK], BF16, name="hid%d" % k, align_bytes=64)
+                    WCOPY[k](hid[:].bitcast(F32).rearrange("p (l u) -> p l u", u=2), words[k][:].rearrange("p (u l) -> p l u", u=2))
+                    codes, scales = quantize(hid[:], Q, "hid%d" % k)
+                    acc = bank(sum_banks[second][k])
+                    nc.tensor.matmul_mx(out=acc[:, 0:Q], lhsT=w3_q[0][:].bitcast(FP8X4), lhsT_scale=w3_q[1][:],
+                                        rhs=codes[:].bitcast(FP8X4), rhs_scale=scales[:], start=True, stop=True)
+                    res = keep.tile([P, Q], F32, name="res%d" % k)
+                    RCOPY[k](res[:], acc[:, 0:Q])
+                    nc.sync.dma_start(out[:, k * Q : (k + 1) * Q], res[:])

@@ -40,19 +40,21 @@ def tile_picked_ytraffs_queue_p_kernel(tc, x_words, x_scales, w1, w2, sat, unit,
 
         ORDER = (2, 3, 0, 1)
         UORD = (1, 0)
-        MERGED = (0, 1)
+        MERGED = ()
         sc, vc = nc.scalar.copy, nc.vector.tensor_copy
         WCOPY = [sc]*4
         RCOPY = [sc]*4
+        RED = False
+        AGAIN = True
         FUSED = (2, 3)
-        OWN_ENG = nc.vector
+        OWN_ENG = nc.gpsimd
         def part_v(dst, src):
             nc.vector.tensor_scalar(dst, src, -0.3, None, ALU.mult)
         def part_s(dst, src):
             nc.scalar.activation(dst, src, ACT.Copy, scale=-0.3)
         def part_g(dst, src):
             nc.gpsimd.tensor_scalar(dst, src, -0.3, 0.0, ALU.mult, ALU.add)
-        PART_ENG = [part_g]*4
+        PART_ENG = [part_s,part_s,part_g,part_g]
         xs_all = keep.tile([P, T], U8, name="xs_all")
         nc.vector.memset(xs_all[:].bitcast(I32), 0)
         offs_t = keep.tile([P, S // 16], U16, name="offs_t")
@@ -143,6 +145,8 @@ def tile_picked_ytraffs_queue_p_kernel(tc, x_words, x_scales, w1, w2, sat, unit,
         w2_q = quantize(w2_bf[:], H, "w2")
         w3_bf = keep.tile([P, N, PACK], BF16, name="w3_bf", align_bytes=64)
         nc.vector.tensor_copy(w3_bf[:], w3_raw[:].rearrange("p j m -> p m j"))
+        unit_pairs = keep.tile([P, 2, P, 2], F32, name="unit_pairs")
+        nc.vector.tensor_copy(unit_pairs[:], unit_row[:].rearrange("l (p u e) -> l u p e", u=2, e=2))
         w3_q = quantize(w3_bf[:].rearrange("p m j -> p (m j)"), N, "w3")
 
         queue = [keep.tile([P, S], F32, name="queue%d" % t) for t in range(PACK)]
@@ -153,7 +157,7 @@ def tile_picked_ytraffs_queue_p_kernel(tc, x_words, x_scales, w1, w2, sat, unit,
             if t in FUSED:
                 OWN_ENG.tensor_scalar(own[t][:], queue[t][:], 1.25, 0.0, ALU.mult, ALU.add)
 
-        press = [keep.tile([P, D, V], F32, name="press%d" % t) for t in range(PACK)]
+        phase = keep.tile([P, PACK, V], F32, name="phase")
         gap = [keep.tile([P, S], F32, name="gap%d" % t) for t in range(PACK)]
         for t in ORDER:
             if t not in FUSED:
@@ -165,36 +169,27 @@ def tile_picked_ytraffs_queue_p_kernel(tc, x_words, x_scales, w1, w2, sat, unit,
                     nc.vector.tensor_tensor(halves(gap[t], h), queue[t][:].indirect(lanes(h)), halves(own[t], h), ALU.subtract)
             else:
                 nc.vector.scalar_tensor_tensor(gap[t][:], queue[t][:], -1.25, gap[t][:], ALU.mult, ALU.add)
-            nc.vector.scalar_tensor_tensor(press[t][:].rearrange("p d v -> p v d"), gap[t][:].rearrange("p (v d) -> p v d", d=D), 0.0,
-                                           sat_t[t][:].rearrange("p (v d) -> p v d", d=D), ALU.min, ALU.mult)
+            nc.vector.scalar_tensor_tensor(gap[t][:], gap[t][:], 0.0, sat_t[t][:], ALU.min, ALU.mult)
+            if RED:
+                nc.vector.tensor_reduce(phase[:, t, :], gap[t][:].rearrange("p (v d) -> p v d", d=D), AXIS.X, ALU.add)
+            else:
+                twos = work.tile([P, HALF], F32, name="twos")
+                nc.vector.tensor_tensor(twos[:], gap[t][:, 0:S:2], gap[t][:, 1:S:2], ALU.add)
+                nc.vector.tensor_tensor(phase[:, t, :], twos[:, 0:HALF:2], twos[:, 1:HALF:2], ALU.add)
 
         oc = sigmoids(w2_q)
         for t in ORDER:
             logarithm(t)
 
-        phase = [bank(b) for b in range(2)]
-        for n, t in enumerate(ORDER):
-            for d in range(D):
-                for b in range(2):
-                    nc.tensor.matmul(phase[b][:, t * P : (t + 1) * P], press[t][:, d, b * P : (b + 1) * P], ident[:],
-                                     start=(n == 0 and d == 0), stop=(n == PACK - 1 and d == D - 1), is_transpose=True)
-        shared = keep.tile([P, 2 * S], F32, name="shared")
-        green_t = shared[:, HALF : HALF + S].rearrange("p (b i) -> p b i", b=2)
-        for b in range(2):
-            nc.scalar.activation(green_t[:, b, :], phase[b][:], ACT.Ln, scale=-0.8 / 1.5, bias=TINY)
-        green = {}
+        green = keep.tile([P, PACK, V], F32, name="green")
+        nc.scalar.activation(green[:], phase[:], ACT.Ln, scale=-0.8 / 1.5, bias=TINY)
         for u in UORD:
-            pair = green_t[:, :, 2 * u * P : (2 * u + 2) * P]
-            nc.scalar.activation(pair, pair, ACT.Sigmoid)
-            green[u] = bank(u)
-            for e in range(2):
-                for b in range(2):
-                    nc.tensor.transpose(green[u][:, (2 * e + b) * P : (2 * e + b + 1) * P], green_t[:, b, (2 * u + e) * P : (2 * u + e + 1) * P], ident[:])
+            nc.scalar.activation(green[:, 2 * u : 2 * u + 2, :], green[:, 2 * u : 2 * u + 2, :], ACT.Sigmoid)
 
         occ = [keep.tile([P, S], F32, name="occ%d" % t) for t in range(PACK)]
         occ_part = [logs[t][:] for t in range(PACK)]
         for t in ORDER:
-            if t < 2:
+            if t < 2 and AGAIN:
                 for h in range(2):
                     oc[t, h] = product(w2_q, t, h, 4 + 2 * t + h)
             softplus_end(occ[t], oc, t)
@@ -208,7 +203,7 @@ def tile_picked_ytraffs_queue_p_kernel(tc, x_words, x_scales, w1, w2, sat, unit,
         for t in ORDER:
             flow = work.tile([P, S], F32, name="flow")
             for h in range(2):
-                share = green[t // 2][:, (t % 2) * V + h * P : (t % 2) * V + (h + 1) * P]
+                share = green[:, t, h * P : (h + 1) * P]
                 nc.vector.scalar_tensor_tensor(
                     halves(flow, h).rearrange("p (v d) -> p v d", d=D), share.unsqueeze(2).to_broadcast([P, P, D]), -1.2,
                     halves(occ[t], h).rearrange("p (v d) -> p v d", d=D), ALU.mult, ALU.mult)
@@ -220,7 +215,7 @@ def tile_picked_ytraffs_queue_p_kernel(tc, x_words, x_scales, w1, w2, sat, unit,
         hid_t = [keep.tile([P, 8, P, 2], BF16, name="hid_t%d" % u) for u in range(2)]
         words = {}
         first, second = UORD
-        sum_banks = {first: (2, 3, 4, 5), second: (6, 7, first, second)}
+        sum_banks = {first: (0, 1, 2, 3), second: (4, 5, 6, 7)} if AGAIN else {first: (4, 5, 6, 7), second: (0, 1, 2, 3)}
         Q = S // 4
         for u in UORD:
             sums = [bank(b) for b in sum_banks[u]]
@@ -242,7 +237,7 @@ def tile_picked_ytraffs_queue_p_kernel(tc, x_words, x_scales, w1, w2, sat, unit,
                 for k in range(4):
                     add_turned(unserved, e, k)
                     add_turned(arrive, e, k, stop=(e == 1))
-            unit_u = unit_row[:].rearrange("l (p u e) -> l u p e", u=2, e=2)[:, u]
+            unit_u = unit_pairs[:, u]
             for k in range(4):
                 nc.vector.tensor_tensor(hid_t[u][:, 2 * k : 2 * k + 2], sums[k][:].rearrange("l (b e p) -> l b p e", b=2, e=2),
                                         unit_u.unsqueeze(1).to_broadcast([P, 2, P, 2]), ALU.mult)

from contextlib import ExitStack

import concourse.mybir as mybir
from concourse.masks import make_identity

K, T, S, D, N, H = 512, 2048, 1024, 4, 128, 512
FLOPS = 2 * K * H * S * 2 + 2 * H * N * S

F32 = mybir.dt.float32
BF16 = mybir.dt.bfloat16
I32 = mybir.dt.int32
U32 = mybir.dt.uint32
U16 = mybir.dt.uint16
U8 = mybir.dt.uint8
FP8X4 = mybir.dt.float8_e4m3fn_x4
ALU = mybir.AluOpType
ACT = mybir.ActivationFunctionType
AXIS = mybir.AxisListType

P = 128
PACK = 4
HALF = S // 2
COLS = HALF // 16
V = S // D
TINY = 2.0 ** -63


def tile_picked_ytraffs_queue_p_kernel(tc, x_words, x_scales, w1, w2, sat, unit, w3, offs, dsn, out):
    nc = tc.nc
    with ExitStack() as ctx:
        keep = ctx.enter_context(tc.tile_pool(name="keep", bufs=1))
        work = ctx.enter_context(tc.tile_pool(name="work", bufs=2))
        psum = ctx.enter_context(tc.psum_pool(name="psum", bufs=1))

        def bank(b):
            return psum.tile([P, 512], F32, name="bank%d" % b, tag="bank%d" % b)

        def halves(ap, h):
            return ap[:, h * HALF : (h + 1) * HALF]

        ORDER = (2, 3, 0, 1)
        UORD = (1, 0)
        MERGED = ()
        sc, vc = nc.scalar.copy, nc.vector.tensor_copy
        WCOPY = [sc]*4
        RCOPY = [sc]*4
        RED = False
        AGAIN = True
        FUSED = (2, 3)
        OWN_ENG = nc.gpsimd
        def part_v(dst, src):
            nc.vector.tensor_scalar(dst, src, -0.3, None, ALU.mult)
        def part_s(dst, src):
            nc.scalar.activation(dst, src, ACT.Copy, scale=-0.3)
        def part_g(dst, src):
            nc.gpsimd.tensor_scalar(dst, src, -0.3, 0.0, ALU.mult, ALU.add)
        PART_ENG = [part_s,part_s,part_g,part_g]
        xs_all = keep.tile([P, T], U8, name="xs_all")
        nc.vector.memset(xs_all[:].bitcast(I32), 0)
        offs_t = keep.tile([P, S // 16], U16, name="offs_t")
        nc.sync.dma_start(offs_t[:], offs)
        for q in range(4):
            nc.sync.dma_start(xs_all[32 * q : 32 * q + 4, :].bitcast(I32), x_scales[0, 4 * q : 4 * q + 4, :].bitcast(I32))
        w1_raw = keep.tile([P, PACK, H], F32, name="w1_raw")
        nc.sync.dma_start(w1_raw[:], w1.rearrange("(p j) c -> p j c", j=PACK))
        xw_all = keep.tile([P, T], I32, name="xw_all")
        nc.sync.dma_start(xw_all[:], x_words[0].rearrange("p n t -> p (n t)").bitcast(I32))
        w2_raw = keep.tile([P, PACK, H], F32, name="w2_raw")
        nc.sync.dma_start(w2_raw[:], w2.rearrange("(p j) c -> p j c", j=PACK))
        dsn_t = keep.tile([P, S // 16], U16, name="dsn_t")
        nc.sync.dma_start(dsn_t[:], dsn)
        sat_rows = sat.rearrange("(p t) j -> p t j", t=PACK)
        sat_t = [keep.tile([P, S], F32, name="sat%d" % t) for t in range(PACK)]
        for t in (2, 3, 0, 1):
            nc.sync.dma_start(sat_t[t][:], sat_rows[:, t, :])
        w3_raw = keep.tile([P, PACK, N], F32, name="w3_raw")
        nc.sync.dma_start(w3_raw[:], w3.rearrange("(p j) c -> p j c", j=PACK))
        unit_row = keep.tile([P, H], F32, name="unit_row")
        nc.sync.dma_start(unit_row[:], unit.rearrange("h o -> (h o)").partition_broadcast(P))

        ident = keep.tile([P, P], F32, name="ident")
        make_identity(nc, ident[:])

        xw = [keep.tile([P, HALF], U32, name="xw%d" % h, align_bytes=64) for h in range(2)]
        xs = [keep.tile([P, HALF], U8, name="xs%d" % h, align_bytes=64) for h in range(2)]

        def pick_scales(h):
            nc.vector.tensor_copy(xs[h][:], xs_all[:].indirect(offs_t[:, h * COLS : (h + 1) * COLS]))

        def pick_words(h):
            nc.vector.tensor_copy(xw[h][:], xw_all[:].bitcast(U32).indirect(offs_t[:, h * COLS : (h + 1) * COLS]))

        def dealt_views(raw, grouped, mh):
            dst = grouped[:].rearrange("p (t m j) -> p m j t", t=PACK, j=PACK)[:, 64 * mh : 64 * mh + 64]
            src = raw[:].rearrange("p j (m t) -> p m j t", t=PACK)[:, 64 * mh : 64 * mh + 64]
            return dst, src

        def quantize(grouped, width, label):
            codes = keep.tile([P, width], U32, name=label + "_codes", align_bytes=64)
            scales = keep.tile([P, width], U8, name=label + "_scales", align_bytes=64)
            nc.vector.quantize_mx(out=codes[:].bitcast(FP8X4), scales=scales[:], in_=grouped)
            return codes, scales

        pick_scales(0)
        w1_bf = keep.tile([P, PACK * H], BF16, name="w1_bf", align_bytes=64)
        nc.scalar.copy(*dealt_views(w1_raw, w1_bf, 0))
        nc.vector.tensor_copy(*dealt_views(w1_raw, w1_bf, 1))
        w1_q = quantize(w1_bf[:], H, "w1")
        pick_words(0)
        pick_scales(1)
        pick_words(1)

        def product(wq, t, h, b):
            acc = bank(b)
            cols = slice(P * t, P * (t + 1))
            nc.tensor.matmul_mx(out=acc[:], lhsT=wq[0][:, cols].bitcast(FP8X4), lhsT_scale=wq[1][:, cols],
                                rhs=xw[h][:].bitcast(FP8X4), rhs_scale=xs[h][:], start=True, stop=True)
            return acc

        logs = [keep.tile([P, S], F32, name="logs%d" % t) for t in range(PACK)]

        def sigmoids(wq):
            accs = {}
            for h in range(2):
                for t in ORDER:
                    accs[t, h] = product(wq, t, h, 2 * t + h)
                    nc.scalar.activation(halves(logs[t], h), accs[t, h][:], ACT.Sigmoid, scale=-1.0)
            return accs

        def logarithm(t):
            nc.scalar.activation(logs[t][:], logs[t][:], ACT.Ln, bias=TINY)

        def softplus_end(dst, accs, t):
            for h in range(2):
                nc.vector.scalar_tensor_tensor(halves(dst, h), halves(logs[t], h), -1.0, accs[t, h][:], ALU.mult, ALU.max)

        def lanes(h):
            return dsn_t[:, h * COLS : (h + 1) * COLS]

        qe = sigmoids(w1_q)

        w2_bf = keep.tile([P, PACK * H], BF16, name="w2_bf", align_bytes=64)
        for mh in range(2):
            nc.vector.tensor_copy(*dealt_views(w2_raw, w2_bf, mh))
        w2_q = quantize(w2_bf[:], H, "w2")
        w3_bf = keep.tile([P, N, PACK], BF16, name="w3_bf", align_bytes=64)
        nc.vector.tensor_copy(w3_bf[:], w3_raw[:].rearrange("p j m -> p m j"))
        unit_pairs = keep.tile([P, 2, P, 2], F32, name="unit_pairs")
        nc.vector.tensor_copy(unit_pairs[:], unit_row[:].rearrange("l (p u e) -> l u p e", u=2, e=2))
        w3_q = quantize(w3_bf[:].rearrange("p m j -> p (m j)"), N, "w3")

        queue = [keep.tile([P, S], F32, name="queue%d" % t) for t in range(PACK)]
        own = {t: keep.tile([P, S], F32, name="own%d" % t) for t in FUSED}
        for t in ORDER:
            logarithm(t)
            softplus_end(queue[t], qe, t)
            if t in FUSED:
                OWN_ENG.tensor_scalar(own[t][:], queue[t][:], 1.25, 0.0, ALU.mult, ALU.add)

        phase = keep.tile([P, PACK, V], F32, name="phase")
        gap = [keep.tile([P, S], F32, name="gap%d" % t) for t in range(PACK)]
        for t in ORDER:
            if t not in FUSED:
                for h in range(2):
                    nc.scalar.activation(halves(gap[t], h), queue[t][:].indirect(lanes(h)), ACT.Copy)
        for t in ORDER:
            if t in FUSED:
                for h in range(2):
                    nc.vector.tensor_tensor(halves(gap[t], h), queue[t][:].indirect(lanes(h)), halves(own[t], h), ALU.subtract)
            else:
                nc.vector.scalar_tensor_tensor(gap[t][:], queue[t][:], -1.25, gap[t][:], ALU.mult, ALU.add)
            nc.vector.scalar_tensor_tensor(gap[t][:], gap[t][:], 0.0, sat_t[t][:], ALU.min, ALU.mult)
            if RED:
                nc.vector.tensor_reduce(phase[:, t, :], gap[t][:].rearrange("p (v d) -> p v d", d=D), AXIS.X, ALU.add)
            else:
                twos = work.tile([P, HALF], F32, name="twos")
                nc.vector.tensor_tensor(twos[:], gap[t][:, 0:S:2], gap[t][:, 1:S:2], ALU.add)
                nc.vector.tensor_tensor(phase[:, t, :], twos[:, 0:HALF:2], twos[:, 1:HALF:2], ALU.add)

        oc = sigmoids(w2_q)
        for t in ORDER:
            logarithm(t)

        green = keep.tile([P, PACK, V], F32, name="green")
        nc.scalar.activation(green[:], phase[:], ACT.Ln, scale=-0.8 / 1.5, bias=TINY)
        for u in UORD:
            nc.scalar.activation(green[:, 2 * u : 2 * u + 2, :], green[:, 2 * u : 2 * u + 2, :], ACT.Sigmoid)

        occ = [keep.tile([P, S], F32, name="occ%d" % t) for t in range(PACK)]
        occ_part = [logs[t][:] for t in range(PACK)]
        for t in ORDER:
            if t < 2 and AGAIN:
                for h in range(2):
                    oc[t, h] = product(w2_q, t, h, 4 + 2 * t + h)
            softplus_end(occ[t], oc, t)
            if t in MERGED:
                nc.vector.scalar_tensor_tensor(occ_part[t], occ[t][:], -0.3, queue[t][:], ALU.mult, ALU.add)
            else:
                PART_ENG[t](occ_part[t], occ[t][:])

        unserved = [keep.tile([P, S], F32, name="unserved%d" % t) for t in range(PACK)]
        arrive = gap
        for t in ORDER:
            flow = work.tile([P, S], F32, name="flow")
            for h in range(2):
                share = green[:, t, h * P : (h + 1) * P]
                nc.vector.scalar_tensor_tensor(
                    halves(flow, h).rearrange("p (v d) -> p v d", d=D), share.unsqueeze(2).to_broadcast([P, P, D]), -1.2,
                    halves(occ[t], h).rearrange("p (v d) -> p v d", d=D), ALU.mult, ALU.mult)
            for h in range(2):
                nc.vector.scalar_tensor_tensor(halves(unserved[t], h), halves(queue[t], h), -1.0, halves(flow, h), ALU.mult, ALU.max)
            for h in range(2):
                nc.scalar.activation(halves(arrive[t], h), unserved[t][:].indirect(lanes(h)), ACT.Copy, scale=-0.5)

        hid_t = [keep.tile([P, 8, P, 2], BF16, name="hid_t%d" % u) for u in range(2)]
        words = {}
        first, second = UORD
        sum_banks = {first: (0, 1, 2, 3), second: (4, 5, 6, 7)} if AGAIN else {first: (4, 5, 6, 7), second: (0, 1, 2, 3)}
        Q = S // 4
        for u in UORD:
            sums = [bank(b) for b in sum_banks[u]]

            def add_turned(terms, e, k, start=False, stop=False):
                for b in range(2):
                    blk = 2 * k + b
                    nc.tensor.matmul(sums[k][:, (2 * b + e) * P : (2 * b + e + 1) * P], terms[2 * u + e][:, blk * P : (blk + 1) * P], ident[:],
                                     start=start and b == 0, stop=stop and b == 1, is_transpose=True)

            for k in range(4):
                for e in range(2):
                    if 2 * u + e not in MERGED:
                        add_turned(queue, e, k, start=(e == 0))
            for e in range(2):
                for k in range(4):
                    add_turned(occ_part, e, k, start=(e == 0 and 2 * u in MERGED))
            for e in range(2):
                for k in range(4):
                    add_turned(unserved, e, k)
                    add_turned(arrive, e, k, stop=(e == 1))
            unit_u = unit_pairs[:, u]
            for k in range(4):
                nc.vector.tensor_tensor(hid_t[u][:, 2 * k : 2 * k + 2], sums[k][:].rearrange("l (b e p) -> l b p e", b=2, e=2),
                                        unit_u.unsqueeze(1).to_broadcast([P, 2, P, 2]), ALU.mult)
                if u == first:
                    words[k] = bank(sum_banks[first][k])
                pairs = hid_t[u][:].rearrange("l b p e -> l (b p e)").bitcast(F32)
                for b in range(2):
                    blk = 2 * k + b
                    nc.tensor.transpose(words[k][:, (2 * u + b) * P : (2 * u + b + 1) * P], pairs[:, blk * P : (blk + 1) * P], ident[:])
                if u == second:
                    hid = keep.tile([P, Q * PACK], BF16, name="hid%d" % k, align_bytes=64)
                    WCOPY[k](hid[:].bitcast(F32).rearrange("p (l u) -> p l u", u=2), words[k][:].rearrange("p (u l) -> p l u", u=2))
                    codes, scales = quantize(hid[:], Q, "hid%d" % k)
                    acc = bank(sum_banks[second][k])
                    nc.tensor.matmul_mx(out=acc[:, 0:Q], lhsT=w3_q[0][:].bitcast(FP8X4), lhsT_scale=w3_q[1][:],
                                        rhs=codes[:].bitcast(FP8X4), rhs_scale=scales[:], start=True, stop=True)
                    res = keep.tile([P, Q], F32, name="res%d" % k)
                    RCOPY[k](res[:], acc[:, 0:Q])
                    nc.sync.dma_start(out[:, k * Q : (k + 1) * Q], res[:])
